import numpy as np
import ml_dtypes


def mxq(x, axis, fmt="e4m3"):
    dtype, down = {"e4m3": (ml_dtypes.float8_e4m3fn, 7), "e5m2": (ml_dtypes.float8_e5m2, 14)}[fmt]
    v = np.moveaxis(np.asarray(x, np.float32).astype(ml_dtypes.bfloat16).astype(np.float64), axis, -1)
    blocks = v.reshape(v.shape[:-1] + (-1, 32))
    amax = np.abs(blocks).max(-1, keepdims=True)
    byte = np.maximum(np.where(amax > 0, np.frexp(amax)[1] - 1 + 127, 0) - down, 1)
    scale = np.exp2(byte - 127.0)
    codes = (blocks / scale).astype(np.float32).astype(dtype).astype(np.float64)
    return np.moveaxis((codes * scale).reshape(v.shape), -1, axis)


WIDE = False


def mx_kscale(k):
    if not WIDE:
        return np.ones(k)
    levels = np.array([10, -10, 5, -5, 0])
    if k % 512:
        return np.exp2(np.random.permutation(np.resize(levels, k // 32))).repeat(32)
    a = np.empty((k // 512, 16))
    for p in range(k // 512):
        a[p, :8] = np.random.permutation(np.resize(levels, 8))
        for g in range(8):
            far = levels[np.abs(levels - a[p, g]) >= 10]
            a[p, g + 8] = far[np.random.randint(len(far))]
    return np.exp2(a.ravel()).repeat(32)


BF16 = ml_dtypes.bfloat16


def bf(x):
    return np.asarray(x, np.float32).astype(BF16)


def f64(x):
    return np.asarray(x).astype(np.float64)


E2M1 = np.array([0.0, 0.5, 1.0, 1.5, 2.0, 3.0, 4.0, 6.0, -0.0, -0.5, -1.0, -1.5, -2.0, -3.0, -4.0, -6.0])


def pack_weight(w, fmt):
    k, n = w.shape
    w = f64(bf(w)).reshape(k // 32, 32, n)
    amax = np.abs(w).max(1)
    if fmt == "e4m3":
        byte = np.frexp(amax)[1] - 1 + 127 - 7
    else:
        mant, ex = np.frexp(amax / 6.0)
        byte = np.where(mant > 0.5, ex, ex - 1) + 127
    byte = np.clip(np.where(amax > 0, byte, 1), 1, 254)
    scaled = (w * np.exp2(127.0 - byte)[:, None, :]).reshape(k, n).astype(np.float32)
    by_word = np.ascontiguousarray(scaled.reshape(k // 512, 128, 4, n).transpose(0, 1, 3, 2))
    if fmt == "e4m3":
        words = by_word.astype(ml_dtypes.float8_e4m3fn).view(np.uint8)
    else:
        c = by_word.astype(ml_dtypes.float4_e2m1fn).view(np.uint8) & 0xF
        words = c[..., 0::2] | (c[..., 1::2] << 4)
    return np.ascontiguousarray(words), np.ascontiguousarray(byte.astype(np.uint8).reshape(k // 512, 16, n))


def unpack_weight(words, scales, fmt):
    g, p, n, _ = words.shape
    if fmt == "e4m3":
        vals = np.ascontiguousarray(words).view(ml_dtypes.float8_e4m3fn).astype(np.float64)
    else:
        nib = np.empty((g, p, n, 4), np.uint8)
        nib[..., 0::2] = words & 0xF
        nib[..., 1::2] = words >> 4
        vals = E2M1[nib]
    vals = vals * np.repeat(np.exp2(scales.astype(np.float64) - 127.0), 8, axis=1)[..., None]
    return vals.transpose(0, 1, 3, 2).reshape(g * 512, n)
def pack4(w):
    words, scales = pack_weight(w, "e2m1")
    return words.reshape(words.shape[0], 128, -1), scales


def unpack4(words, scales):
    return unpack_weight(words.reshape(words.shape[0], 128, -1, 2), scales, "e2m1")


M, N = 1536, 1024
OMEGA1, OMEGA2 = 0.9, 0.6
CENTRE = 1.0 + OMEGA1 / OMEGA2 - OMEGA1


def setup_inputs():
    s = mx_kscale(N)
    dinv = np.exp(0.3 * np.random.standard_normal(N))
    off = (1.0 - np.eye(N)) / np.sqrt(3 * N) / s[:, None]
    far = np.random.standard_normal((N, N)) * off
    near = np.random.standard_normal((N, N)) * off
    fresh = np.random.standard_normal((N, N)) * off
    far_words, far_scales = pack4(far)
    near_words, near_scales = pack_weight(near, "e4m3")
    return {"b": bf(np.random.standard_normal((M, N))),
            "relax1": bf(OMEGA1 * dinv * s),
            "relax2": bf(OMEGA2 * dinv),
            "far_words": far_words, "far_scales": far_scales,
            "near_words": near_words, "near_scales": near_scales,
            "fresh": bf(fresh)}


def reference(b, relax1, relax2, far_words, far_scales, near_words, near_scales, fresh):
    rhs = f64(b)
    x1 = mxq(rhs * f64(relax1), 1, "e4m3")
    y_far = x1 @ unpack4(far_words, far_scales)
    y_near = x1 @ unpack_weight(near_words, near_scales, "e4m3")
    y_fresh = x1 @ mxq(f64(fresh), 0, "e4m3")
    return (CENTRE * rhs - y_far - y_near - y_fresh) * f64(relax2)

@@ -1,0 +1,314 @@
+from contextlib import ExitStack
+
+import concourse.mybir as mybir
+from concourse.masks import make_identity
+
+M, N = 1536, 1024
+CENTRE = 1.6
+FLOPS = 3 * 2 * M * N * N
+
+F32 = mybir.dt.float32
+BF16 = mybir.dt.bfloat16
+I32 = mybir.dt.int32
+U32 = mybir.dt.uint32
+U8 = mybir.dt.uint8
+FP8X4 = mybir.dt.float8_e4m3fn_x4
+FP4X4 = mybir.dt.float4_e2m1fn_x4
+ALU = mybir.AluOpType
+
+P = 128
+G = 2
+HALF = 512
+TILES = M // P
+
+
+def tile_two_jacobi_sweeps_s10_kernel(
+    tc, b, relax1, relax2, far_words, far_scales, near_words, near_scales, fresh, out
+):
+    nc = tc.nc
+    with ExitStack() as ctx:
+        keep = ctx.enter_context(tc.tile_pool(name="keep", bufs=1))
+        work = ctx.enter_context(tc.tile_pool(name="work", bufs=3))
+        turned = ctx.enter_context(tc.psum_pool(name="turned", bufs=2))
+        sums = ctx.enter_context(tc.psum_pool(name="sums", bufs=6))
+        ctx.enter_context(tc.manual_schedule())
+
+        ident = keep.tile([P, P], F32, name="ident")
+        make_identity(nc, ident[:])
+
+        far_sc = keep.tile([P, G * N], U8, name="far_sc", align_bytes=64)
+        near_sc = keep.tile([P, G * N], U8, name="near_sc", align_bytes=64)
+        nc.vector.memset(far_sc[:].bitcast(I32), 0)
+        nc.vector.memset(near_sc[:].bitcast(I32), 0)
+
+        r1c = keep.tile([P, G, 2, 2], BF16, name="r1c", align_bytes=64)
+        r2c = keep.tile([P, G * 4], BF16, name="r2c", align_bytes=64)
+        r2 = keep.tile([P, N], BF16, name="r2", align_bytes=64)
+
+        b_sb = {}
+
+        def load_b(i):
+            b_sb[i] = keep.tile([P, N], BF16, name="b%d" % i, align_bytes=64)
+            nc.sync.dma_start(out=b_sb[i][:], in_=b[i * P : (i + 1) * P, :])
+
+        def load_scales(eng, plane, dram):
+            words = plane[:].bitcast(I32)
+            src = dram.bitcast(I32)
+            for q in range(4):
+                eng.dma_start(
+                    out=words[32 * q : 32 * q + 4, :].rearrange("r (g n) -> r g n", g=G),
+                    in_=src[:, 4 * q : 4 * q + 4, :].rearrange("g r n -> r g n"),
+                )
+
+        far = {}
+        near = {}
+        raw = {}
+
+        def load_far(h):
+            far[h] = keep.tile([P, G, 2 * HALF], U8, name="far%d" % h, align_bytes=64)
+            nc.sync.dma_start(
+                out=far[h][:],
+                in_=far_words[:, :, h * 2 * HALF : (h + 1) * 2 * HALF].rearrange("g p c -> p g c"),
+            )
+
+        def load_near(h):
+            near[h] = keep.tile([P, G, 4 * HALF], U8, name="near%d" % h, align_bytes=64)
+            nc.sync.dma_start(
+                out=near[h][:],
+                in_=near_words[:, :, h * HALF : (h + 1) * HALF, :].rearrange("g p n t -> p g (n t)"),
+            )
+
+        def load_fresh(g, h):
+            raw[g, h] = keep.tile([P, 4, HALF], BF16, name="raw%d%d" % (g, h), align_bytes=64)
+            nc.sync.dma_start(
+                out=raw[g, h][:],
+                in_=fresh[g * 512 : (g + 1) * 512, h * HALF : (h + 1) * HALF].rearrange("(p j) n -> p j n", j=4),
+            )
+
+        load_b(0)
+        nc.scalar.dma_start(
+            out=r1c[:], in_=relax1.rearrange("(g p u e) -> p g u e", g=G, u=2, e=2)
+        )
+        load_scales(nc.scalar, far_sc, far_scales)
+        load_far(0)
+        load_b(1)
+        load_scales(nc.scalar, near_sc, near_scales)
+        load_near(0)
+        load_b(2)
+        load_b(3)
+        nc.scalar.dma_start(
+            out=r2c[:].rearrange("p (g s) -> p g s", g=G),
+            in_=relax2.rearrange("(g p s) -> p g s", g=G, s=4),
+        )
+        load_fresh(0, 0)
+        load_fresh(1, 0)
+        load_far(1)
+        load_near(1)
+        load_b(4)
+        load_b(5)
+        load_fresh(0, 1)
+        load_fresh(1, 1)
+        for i in range(6, TILES):
+            load_b(i)
+
+        words_in = {}
+
+        def permute(i):
+            t = work.tile([P, 2 * P * G], F32, name="perm", align_bytes=64)
+            nc.scalar.copy(
+                out=t[:].rearrange("m (g u p) -> m g u p", g=G, u=2),
+                in_=b_sb[i][:].bitcast(F32).rearrange("m (g p u) -> m g u p", g=G, u=2),
+            )
+            words_in[i] = t
+
+        tr = {}
+
+        def turn(i):
+            bank = turned.tile([P, 512], F32, name="turn")
+            for g in range(G):
+                for u in range(2):
+                    if i in words_in:
+                        src = words_in[i][:, (2 * g + u) * P : (2 * g + u + 1) * P]
+                    else:
+                        src = b_sb[i][:].bitcast(F32)[:, 256 * g + u : 256 * (g + 1) : 2]
+                    nc.tensor.transpose(
+                        bank[:, u * 256 + g * P : u * 256 + (g + 1) * P], src, ident[:]
+                    )
+            tr[i] = bank
+
+        xg = {}
+        xc = {}
+        xs = {}
+
+        def relax(i):
+            t = work.tile([P, G * P * 4], BF16, name="xg", align_bytes=64)
+            nc.vector.tensor_tensor(
+                out=t[:].rearrange("p (g m u e) -> p g m u e", g=G, u=2, e=2),
+                in0=tr[i][:].bitcast(BF16).rearrange("p (u g m e) -> p g m u e", g=G, u=2, e=2),
+                in1=r1c[:].unsqueeze(2).to_broadcast([P, G, P, 2, 2]),
+                op=ALU.mult,
+            )
+            xg[i] = t
+
+        def quantize_x(i):
+            xc[i] = keep.tile([P, G * P], U32, name="xc%d" % i, align_bytes=64)
+            xs[i] = keep.tile([P, G * P], U8, name="xs%d" % i, align_bytes=64)
+            nc.vector.quantize_mx(out=xc[i][:].bitcast(FP8X4), scales=xs[i][:], in_=xg[i][:])
+
+        fi = {}
+        fc = {}
+        fs = {}
+
+        def interleave(eng_copy, g, h):
+            t = work.tile([P, 4 * HALF], BF16, name="fi", align_bytes=64)
+            eng_copy(
+                out=t[:].rearrange("p (c i j) -> p c j i", i=4, j=4),
+                in_=raw[g, h][:].rearrange("p j (c i) -> p c j i", i=4),
+            )
+            fi[g, h] = t
+
+        def quantize_fresh(g, h):
+            fc[g, h] = keep.tile([P, HALF], U32, name="fc%d%d" % (g, h), align_bytes=64)
+            fs[g, h] = keep.tile([P, HALF], U8, name="fs%d%d" % (g, h), align_bytes=64)
+            nc.vector.quantize_mx(out=fc[g, h][:].bitcast(FP8X4), scales=fs[g, h][:], in_=fi[g, h][:])
+
+        acc = {}
+
+        def mm(i, h, part):
+            if part == 0:
+                acc[i, h] = sums.tile([P, HALF], F32, name="acc")
+            for g in range(G):
+                if part == 0:
+                    rhs = far[h][:, g, :].bitcast(FP4X4)
+                    sc = far_sc[:, g * N + h * HALF : g * N + (h + 1) * HALF]
+                elif part == 1:
+                    rhs = near[h][:, g, :].bitcast(FP8X4)
+                    sc = near_sc[:, g * N + h * HALF : g * N + (h + 1) * HALF]
+                else:
+                    rhs = fc[g, h][:].bitcast(FP8X4)
+                    sc = fs[g, h][:]
+                nc.tensor.matmul_mx(
+                    out=acc[i, h][:],
+                    lhsT=xc[i][:, g * P : (g + 1) * P].bitcast(FP8X4),
+                    lhsT_scale=xs[i][:, g * P : (g + 1) * P],
+                    rhs=rhs,
+                    rhs_scale=sc,
+                    start=(part == 0 and g == 0),
+                    stop=(part == 2 and g == 1),
+                )
+
+        late = []
+
+        def e1(i, h, c0, c1):
+            t = work.tile([P, HALF], F32, name="diff", bufs=4)
+            nc.vector.scalar_tensor_tensor(
+                out=t[:, c0:c1],
+                in0=b_sb[i][:, h * HALF + c0 : h * HALF + c1],
+                scalar=CENTRE,
+                in1=acc[i, h][:, c0:c1],
+                op0=ALU.mult,
+                op1=ALU.subtract,
+            )
+            late.append((t, i, h, c0, c1))
+
+        def e2():
+            t, i, h, c0, c1 = late[0]
+            late.remove(late[0])
+            o = work.tile([P, HALF], F32, name="res", bufs=6)
+            nc.vector.tensor_tensor(
+                out=o[:, c0:c1], in0=t[:, c0:c1], in1=r2[:, h * HALF + c0 : h * HALF + c1], op=ALU.mult
+            )
+            nc.sync.dma_start(
+                out=out[i * P : (i + 1) * P, h * HALF + c0 : h * HALF + c1], in_=o[:, c0:c1]
+            )
+
+        def finish(i, h):
+            e1(i, h, 0, HALF)
+            if len(late) > 1:
+                e2()
+
+        turn(0)
+        relax(0)
+        quantize_x(0)
+        turn(1)
+        relax(1)
+        quantize_x(1)
+        permute(2)
+        permute(3)
+        mm(0, 0, 0)
+        mm(1, 0, 0)
+        turn(2)
+        turn(3)
+        relax(2)
+        relax(3)
+        quantize_x(2)
+        quantize_x(3)
+        interleave(nc.scalar.copy, 0, 0)
+        interleave(nc.vector.tensor_copy, 1, 0)
+        quantize_fresh(0, 0)
+        quantize_fresh(1, 0)
+        mm(0, 0, 1)
+        mm(1, 0, 1)
+        for i in (2, 3):
+            mm(i, 0, 0)
+            mm(i, 0, 1)
+
+        bank = turned.tile([P, 512], F32, name="turn")
+        for c in range(4):
+            nc.tensor.transpose(
+                bank[:, c * P : (c + 1) * P],
+                r2c[:].bitcast(F32)[:, c : c + 1].to_broadcast([P, P]),
+                ident[:],
+            )
+        nc.scalar.copy(
+            out=r2[:].bitcast(F32).rearrange("m (g p u) -> m g p u", g=G, u=2),
+            in_=bank[:].rearrange("m (g u p) -> m g p u", g=G, u=2),
+        )
+        permute(4)
+        permute(5)
+        interleave(nc.scalar.copy, 0, 1)
+        interleave(nc.scalar.copy, 1, 1)
+
+        for i in range(4):
+            mm(i, 0, 2)
+            finish(i, 0)
+        turn(4)
+        turn(5)
+        for i in range(4):
+            mm(i, 1, 0)
+            mm(i, 1, 1)
+        relax(4)
+        relax(5)
+        quantize_x(4)
+        quantize_x(5)
+        quantize_fresh(0, 1)
+        quantize_fresh(1, 1)
+        for i in range(3):
+            mm(i, 1, 2)
+            finish(i, 1)
+        mm(3, 1, 2)
+        waiting = (3, 1)
+        for i in range(6, TILES):
+            permute(i)
+        for a in range(4, TILES, 2):
+            nxt = [i for i in (a + 2, a + 3) if i < TILES]
+            for i in nxt:
+                turn(i)
+            for i in nxt:
+                relax(i)
+            finish(waiting[0], waiting[1])
+            for i in nxt:
+                quantize_x(i)
+            for h in range(2):
+                for i in (a, a + 1):
+                    for part in range(3):
+                        mm(i, h, part)
+                    if (i, h) != (a + 1, 1):
+                        finish(i, h)
+            waiting = (a + 1, 1)
+        i, h = waiting
+        e1(i, h, 0, 256)
+        e2()
+        e1(i, h, 256, 512)
+        e2()
+        e2()

@@ -47,9 +47,13 @@ def tile_two_jacobi_sweeps_s10_kernel(
 
         b_sb = {}
 
-        def load_b(i):
-            b_sb[i] = keep.tile([P, N], BF16, name="b%d" % i, align_bytes=64)
-            nc.sync.dma_start(out=b_sb[i][:], in_=b[i * P : (i + 1) * P, :])
+        def load_b(i, count):
+            t = keep.tile([P, count, N], BF16, name="b%d" % i, align_bytes=64)
+            nc.sync.dma_start(
+                out=t[:], in_=b[i * P : (i + count) * P, :].rearrange("(c p) k -> p c k", p=P)
+            )
+            for c in range(count):
+                b_sb[i + c] = t[:, c, :]
 
         def load_scales(eng, plane, dram):
             words = plane[:].bitcast(I32)
@@ -60,16 +64,10 @@ def tile_two_jacobi_sweeps_s10_kernel(
                     in_=src[:, 4 * q : 4 * q + 4, :].rearrange("g r n -> r g n"),
                 )
 
-        far = {}
         near = {}
         raw = {}
 
-        def load_far(h):
-            far[h] = keep.tile([P, G, 2 * HALF], U8, name="far%d" % h, align_bytes=64)
-            nc.sync.dma_start(
-                out=far[h][:],
-                in_=far_words[:, :, h * 2 * HALF : (h + 1) * 2 * HALF].rearrange("g p c -> p g c"),
-            )
+        far_sb = keep.tile([P, G, 2 * N], U8, name="far_sb", align_bytes=64)
 
         def load_near(h):
             near[h] = keep.tile([P, G, 4 * HALF], U8, name="near%d" % h, align_bytes=64)
@@ -85,31 +83,28 @@ def tile_two_jacobi_sweeps_s10_kernel(
                 in_=fresh[g * 512 : (g + 1) * 512, h * HALF : (h + 1) * HALF].rearrange("(p j) n -> p j n", j=4),
             )
 
-        load_b(0)
+        load_b(0, 1)
         nc.scalar.dma_start(
             out=r1c[:], in_=relax1.rearrange("(g p u e) -> p g u e", g=G, u=2, e=2)
         )
-        load_scales(nc.scalar, far_sc, far_scales)
-        load_far(0)
-        load_b(1)
-        load_scales(nc.scalar, near_sc, near_scales)
-        load_near(0)
-        load_b(2)
-        load_b(3)
-        nc.scalar.dma_start(
+        load_scales(nc.sync, far_sc, far_scales)
+        load_b(1, 1)
+        nc.sync.dma_start(out=far_sb[:], in_=far_words.rearrange("g p c -> p g c"))
+        nc.gpsimd.dma_start(
             out=r2c[:].rearrange("p (g s) -> p g s", g=G),
             in_=relax2.rearrange("(g p s) -> p g s", g=G, s=4),
         )
+        load_scales(nc.scalar, near_sc, near_scales)
+        load_near(0)
+        load_b(2, 2)
         load_fresh(0, 0)
         load_fresh(1, 0)
-        load_far(1)
         load_near(1)
-        load_b(4)
-        load_b(5)
+        load_b(4, 2)
         load_fresh(0, 1)
         load_fresh(1, 1)
-        for i in range(6, TILES):
-            load_b(i)
+        for i in range(6, TILES, 2):
+            load_b(i, 2)
 
         words_in = {}
 
@@ -117,7 +112,7 @@ def tile_two_jacobi_sweeps_s10_kernel(
             t = work.tile([P, 2 * P * G], F32, name="perm", align_bytes=64)
             nc.scalar.copy(
                 out=t[:].rearrange("m (g u p) -> m g u p", g=G, u=2),
-                in_=b_sb[i][:].bitcast(F32).rearrange("m (g p u) -> m g u p", g=G, u=2),
+                in_=b_sb[i].bitcast(F32).rearrange("m (g p u) -> m g u p", g=G, u=2),
             )
             words_in[i] = t
 
@@ -125,35 +120,47 @@ def tile_two_jacobi_sweeps_s10_kernel(
 
         def turn(i):
             bank = turned.tile([P, 512], F32, name="turn")
+            tr[i] = bank
             for g in range(G):
                 for u in range(2):
                     if i in words_in:
                         src = words_in[i][:, (2 * g + u) * P : (2 * g + u + 1) * P]
                     else:
-                        src = b_sb[i][:].bitcast(F32)[:, 256 * g + u : 256 * (g + 1) : 2]
+                        src = b_sb[i].bitcast(F32)[:, 256 * g + u : 256 * (g + 1) : 2]
                     nc.tensor.transpose(
                         bank[:, u * 256 + g * P : u * 256 + (g + 1) * P], src, ident[:]
                     )
-            tr[i] = bank
 
         xg = {}
         xc = {}
         xs = {}
 
-        def relax(i):
-            t = work.tile([P, G * P * 4], BF16, name="xg", align_bytes=64)
+        def relax(i, gs=(0, G)):
+            if gs[0] == 0:
+                xg[i] = work.tile([P, G * P * 4], BF16, name="xg", align_bytes=64)
+            n = gs[1] - gs[0]
+            part = slice(gs[0], gs[1])
             nc.vector.tensor_tensor(
-                out=t[:].rearrange("p (g m u e) -> p g m u e", g=G, u=2, e=2),
-                in0=tr[i][:].bitcast(BF16).rearrange("p (u g m e) -> p g m u e", g=G, u=2, e=2),
-                in1=r1c[:].unsqueeze(2).to_broadcast([P, G, P, 2, 2]),
+                out=xg[i][:, gs[0] * 512 : gs[1] * 512].rearrange(
+                    "p (g m u e) -> p g m u e", g=n, u=2, e=2
+                ),
+                in0=tr[i][:]
+                .bitcast(BF16)
+                .rearrange("p (u g m e) -> p g m u e", g=G, u=2, e=2)[:, part],
+                in1=r1c[:, part].unsqueeze(2).to_broadcast([P, n, P, 2, 2]),
                 op=ALU.mult,
             )
-            xg[i] = t
 
-        def quantize_x(i):
-            xc[i] = keep.tile([P, G * P], U32, name="xc%d" % i, align_bytes=64)
-            xs[i] = keep.tile([P, G * P], U8, name="xs%d" % i, align_bytes=64)
-            nc.vector.quantize_mx(out=xc[i][:].bitcast(FP8X4), scales=xs[i][:], in_=xg[i][:])
+        def quantize_x(i, gs=(0, G)):
+            if gs[0] == 0:
+                xc[i] = keep.tile([P, G * P], U32, name="xc%d" % i, align_bytes=64)
+                xs[i] = keep.tile([P, G * P], U8, name="xs%d" % i, align_bytes=64)
+            cols = slice(gs[0] * P, gs[1] * P)
+            nc.vector.quantize_mx(
+                out=xc[i][:, cols].bitcast(FP8X4),
+                scales=xs[i][:, cols],
+                in_=xg[i][:, gs[0] * 512 : gs[1] * 512],
+            )
 
         fi = {}
         fc = {}
@@ -179,7 +186,7 @@ def tile_two_jacobi_sweeps_s10_kernel(
                 acc[i, h] = sums.tile([P, HALF], F32, name="acc")
             for g in range(G):
                 if part == 0:
-                    rhs = far[h][:, g, :].bitcast(FP4X4)
+                    rhs = far_sb[:, g, h * N : (h + 1) * N].bitcast(FP4X4)
                     sc = far_sc[:, g * N + h * HALF : g * N + (h + 1) * HALF]
                 elif part == 1:
                     rhs = near[h][:, g, :].bitcast(FP8X4)
@@ -228,22 +235,33 @@ def tile_two_jacobi_sweeps_s10_kernel(
                 e2()
 
         turn(0)
-        relax(0)
-        quantize_x(0)
+        relax(0, (0, 1))
+        relax(0, (1, 2))
+        quantize_x(0, (0, 1))
+        quantize_x(0, (1, 2))
         turn(1)
         relax(1)
         quantize_x(1)
-        permute(2)
-        permute(3)
         mm(0, 0, 0)
         mm(1, 0, 0)
         turn(2)
         turn(3)
+        bank = sums.tile([P, 512], F32, name="acc")
+        for c in range(4):
+            nc.tensor.transpose(
+                bank[:, c * P : (c + 1) * P],
+                r2c[:].bitcast(F32)[:, c : c + 1].to_broadcast([P, P]),
+                ident[:],
+            )
         relax(2)
         relax(3)
         quantize_x(2)
         quantize_x(3)
         interleave(nc.scalar.copy, 0, 0)
+        nc.scalar.copy(
+            out=r2[:].bitcast(F32).rearrange("m (g p u) -> m g p u", g=G, u=2),
+            in_=bank[:].rearrange("m (g u p) -> m g p u", g=G, u=2),
+        )
         interleave(nc.vector.tensor_copy, 1, 0)
         quantize_fresh(0, 0)
         quantize_fresh(1, 0)
@@ -252,18 +270,6 @@ def tile_two_jacobi_sweeps_s10_kernel(
         for i in (2, 3):
             mm(i, 0, 0)
             mm(i, 0, 1)
-
-        bank = turned.tile([P, 512], F32, name="turn")
-        for c in range(4):
-            nc.tensor.transpose(
-                bank[:, c * P : (c + 1) * P],
-                r2c[:].bitcast(F32)[:, c : c + 1].to_broadcast([P, P]),
-                ident[:],
-            )
-        nc.scalar.copy(
-            out=r2[:].bitcast(F32).rearrange("m (g p u) -> m g p u", g=G, u=2),
-            in_=bank[:].rearrange("m (g u p) -> m g p u", g=G, u=2),
-        )
         permute(4)
         permute(5)
         interleave(nc.scalar.copy, 0, 1)
@@ -306,9 +312,9 @@ def tile_two_jacobi_sweeps_s10_kernel(
                     if (i, h) != (a + 1, 1):
                         finish(i, h)
             waiting = (a + 1, 1)
+        e2()
         i, h = waiting
         e1(i, h, 0, 256)
-        e2()
         e1(i, h, 256, 512)
         e2()
         e2()

@@ -234,6 +234,42 @@ def tile_two_jacobi_sweeps_s10_kernel(
             if len(late) > 1:
                 e2()
 
+        def quarter(i, h, c):
+            bank = sums.tile([P, HALF], F32, name="acc")
+            for part in range(3):
+                for g in range(G):
+                    c0 = h * HALF + c * P
+                    if part == 0:
+                        rhs = far_sb[:, g, 2 * c0 : 2 * (c0 + P)].bitcast(FP4X4)
+                        sc = far_sc[:, g * N + c0 : g * N + c0 + P]
+                    elif part == 1:
+                        rhs = near[h][:, g, 4 * c * P : 4 * (c + 1) * P].bitcast(FP8X4)
+                        sc = near_sc[:, g * N + c0 : g * N + c0 + P]
+                    else:
+                        rhs = fc[g, h][:, c * P : (c + 1) * P].bitcast(FP8X4)
+                        sc = fs[g, h][:, c * P : (c + 1) * P]
+                    nc.tensor.matmul_mx(
+                        out=bank[:, 0:P],
+                        lhsT=xc[i][:, g * P : (g + 1) * P].bitcast(FP8X4),
+                        lhsT_scale=xs[i][:, g * P : (g + 1) * P],
+                        rhs=rhs,
+                        rhs_scale=sc,
+                        start=(part == 0 and g == 0),
+                        stop=(part == 2 and g == 1),
+                    )
+            t = work.tile([P, HALF], F32, name="diff", bufs=4)
+            nc.vector.scalar_tensor_tensor(
+                out=t[:, c * P : (c + 1) * P],
+                in0=b_sb[i][:, h * HALF + c * P : h * HALF + (c + 1) * P],
+                scalar=CENTRE,
+                in1=bank[:, 0:P],
+                op0=ALU.mult,
+                op1=ALU.subtract,
+            )
+            late.append((t, i, h, c * P, (c + 1) * P))
+            if len(late) > 1:
+                e2()
+
         turn(0)
         relax(0, (0, 1))
         relax(0, (1, 2))
@@ -275,12 +311,16 @@ def tile_two_jacobi_sweeps_s10_kernel(
         interleave(nc.scalar.copy, 0, 1)
         interleave(nc.scalar.copy, 1, 1)
 
+        for i in range(2):
+            mm(i, 1, 0)
         for i in range(4):
             mm(i, 0, 2)
             finish(i, 0)
         turn(4)
         turn(5)
-        for i in range(4):
+        for i in range(2):
+            mm(i, 1, 1)
+        for i in (2, 3):
             mm(i, 1, 0)
             mm(i, 1, 1)
         relax(4)
@@ -289,32 +329,41 @@ def tile_two_jacobi_sweeps_s10_kernel(
         quantize_x(5)
         quantize_fresh(0, 1)
         quantize_fresh(1, 1)
-        for i in range(3):
-            mm(i, 1, 2)
-            finish(i, 1)
-        mm(3, 1, 2)
-        waiting = (3, 1)
+        for i in (4, 5):
+            for part in range(3):
+                mm(i, 0, part)
+            finish(i, 0)
         for i in range(6, TILES):
             permute(i)
-        for a in range(4, TILES, 2):
-            nxt = [i for i in (a + 2, a + 3) if i < TILES]
-            for i in nxt:
-                turn(i)
-            for i in nxt:
-                relax(i)
+        for i in range(4):
+            mm(i, 1, 2)
+            if i < 3:
+                finish(i, 1)
+        waiting = (3, 1)
+        order = [(4, 1), (5, 1)]
+        for a in range(6, TILES, 2):
+            turn(a)
+            turn(a + 1)
+            relax(a)
+            relax(a + 1)
             finish(waiting[0], waiting[1])
-            for i in nxt:
-                quantize_x(i)
-            for h in range(2):
-                for i in (a, a + 1):
-                    for part in range(3):
-                        mm(i, h, part)
-                    if (i, h) != (a + 1, 1):
-                        finish(i, h)
-            waiting = (a + 1, 1)
+            quantize_x(a)
+            quantize_x(a + 1)
+            for i, h in order:
+                for part in range(3):
+                    mm(i, h, part)
+                if (i, h) != order[-1]:
+                    finish(i, h)
+            waiting = order[-1]
+            order = [(a, 0), (a + 1, 0), (a, 1), (a + 1, 1)]
+        finish(waiting[0], waiting[1])
         e2()
-        i, h = waiting
-        e1(i, h, 0, 256)
-        e1(i, h, 256, 512)
-        e2()
+        for i, h in order[:3]:
+            for part in range(3):
+                mm(i, h, part)
+            e1(i, h, 0, HALF)
+            e2()
+        i, h = order[3]
+        for c in range(4):
+            quarter(i, h, c)
         e2()

@@ -42,8 +42,8 @@ def tile_two_jacobi_sweeps_s10_kernel(
         nc.vector.memset(near_sc[:].bitcast(I32), 0)
 
         r1c = keep.tile([P, G, 2, 2], BF16, name="r1c", align_bytes=64)
-        r2c = keep.tile([P, G * 4], BF16, name="r2c", align_bytes=64)
-        r2 = keep.tile([P, N], BF16, name="r2", align_bytes=64)
+        r2c = keep.tile([P, 4, 2], BF16, name="r2c", align_bytes=64)
+        r2 = keep.tile([P, N], F32, name="r2", align_bytes=64)
 
         b_sb = {}
 
@@ -91,8 +91,7 @@ def tile_two_jacobi_sweeps_s10_kernel(
         load_b(1, 1)
         nc.sync.dma_start(out=far_sb[:], in_=far_words.rearrange("g p c -> p g c"))
         nc.gpsimd.dma_start(
-            out=r2c[:].rearrange("p (g s) -> p g s", g=G),
-            in_=relax2.rearrange("(g p s) -> p g s", g=G, s=4),
+            out=r2c[:], in_=relax2.rearrange("(c p e) -> p c e", p=P, e=2)
         )
         load_scales(nc.scalar, near_sc, near_scales)
         load_near(0)
@@ -136,7 +135,7 @@ def tile_two_jacobi_sweeps_s10_kernel(
         xs = {}
 
         def relax(i, gs=(0, G)):
-            if gs[0] == 0:
+            if i not in xg:
                 xg[i] = work.tile([P, G * P * 4], BF16, name="xg", align_bytes=64)
             n = gs[1] - gs[0]
             part = slice(gs[0], gs[1])
@@ -161,6 +160,24 @@ def tile_two_jacobi_sweeps_s10_kernel(
                 scales=xs[i][:, cols],
                 in_=xg[i][:, gs[0] * 512 : gs[1] * 512],
             )
+
+        def relax_pair(a):
+            t = work.tile([P, 2, G * P * 4], BF16, name="xg2", align_bytes=64, bufs=2)
+            xg[a] = t[:, 0, :]
+            xg[a + 1] = t[:, 1, :]
+            relax(a)
+            relax(a + 1)
+            return t
+
+        def quantize_pair(a, t):
+            c = keep.tile([P, 2 * G * P], U32, name="xc%d" % a, align_bytes=64)
+            s = keep.tile([P, 2 * G * P], U8, name="xs%d" % a, align_bytes=64)
+            nc.vector.quantize_mx(
+                out=c[:].bitcast(FP8X4), scales=s[:], in_=t[:].rearrange("p c w -> p (c w)")
+            )
+            for k in range(2):
+                xc[a + k] = c[:, k * G * P : (k + 1) * G * P]
+                xs[a + k] = s[:, k * G * P : (k + 1) * G * P]
 
         fi = {}
         fc = {}
@@ -207,7 +224,7 @@ def tile_two_jacobi_sweeps_s10_kernel(
         late = []
 
         def e1(i, h, c0, c1):
-            t = work.tile([P, HALF], F32, name="diff", bufs=4)
+            t = work.tile([P, HALF], F32, name="diff", bufs=8)
             nc.vector.scalar_tensor_tensor(
                 out=t[:, c0:c1],
                 in0=b_sb[i][:, h * HALF + c0 : h * HALF + c1],
@@ -218,11 +235,11 @@ def tile_two_jacobi_sweeps_s10_kernel(
             )
             late.append((t, i, h, c0, c1))
 
-        def e2():
+        def e2(eng=nc.gpsimd):
             t, i, h, c0, c1 = late[0]
             late.remove(late[0])
             o = work.tile([P, HALF], F32, name="res", bufs=6)
-            nc.vector.tensor_tensor(
+            eng.tensor_tensor(
                 out=o[:, c0:c1], in0=t[:, c0:c1], in1=r2[:, h * HALF + c0 : h * HALF + c1], op=ALU.mult
             )
             nc.sync.dma_start(
@@ -231,10 +248,9 @@ def tile_two_jacobi_sweeps_s10_kernel(
 
         def finish(i, h):
             e1(i, h, 0, HALF)
-            if len(late) > 1:
-                e2()
+            e2()
 
-        def quarter(i, h, c):
+        def quarter(i, h, c, t):
             bank = sums.tile([P, HALF], F32, name="acc")
             for part in range(3):
                 for g in range(G):
@@ -257,7 +273,6 @@ def tile_two_jacobi_sweeps_s10_kernel(
                         start=(part == 0 and g == 0),
                         stop=(part == 2 and g == 1),
                     )
-            t = work.tile([P, HALF], F32, name="diff", bufs=4)
             nc.vector.scalar_tensor_tensor(
                 out=t[:, c * P : (c + 1) * P],
                 in0=b_sb[i][:, h * HALF + c * P : h * HALF + (c + 1) * P],
@@ -266,9 +281,6 @@ def tile_two_jacobi_sweeps_s10_kernel(
                 op0=ALU.mult,
                 op1=ALU.subtract,
             )
-            late.append((t, i, h, c * P, (c + 1) * P))
-            if len(late) > 1:
-                e2()
 
         turn(0)
         relax(0, (0, 1))
@@ -286,7 +298,7 @@ def tile_two_jacobi_sweeps_s10_kernel(
         for c in range(4):
             nc.tensor.transpose(
                 bank[:, c * P : (c + 1) * P],
-                r2c[:].bitcast(F32)[:, c : c + 1].to_broadcast([P, P]),
+                r2c[:].rearrange("p c e -> p (c e)").bitcast(F32)[:, c : c + 1].to_broadcast([P, P]),
                 ident[:],
             )
         relax(2)
@@ -294,10 +306,7 @@ def tile_two_jacobi_sweeps_s10_kernel(
         quantize_x(2)
         quantize_x(3)
         interleave(nc.scalar.copy, 0, 0)
-        nc.scalar.copy(
-            out=r2[:].bitcast(F32).rearrange("m (g p u) -> m g p u", g=G, u=2),
-            in_=bank[:].rearrange("m (g u p) -> m g p u", g=G, u=2),
-        )
+        nc.scalar.copy(out=r2[:], in_=bank[:].bitcast(BF16))
         interleave(nc.vector.tensor_copy, 1, 0)
         quantize_fresh(0, 0)
         quantize_fresh(1, 0)
@@ -323,10 +332,8 @@ def tile_two_jacobi_sweeps_s10_kernel(
         for i in (2, 3):
             mm(i, 1, 0)
             mm(i, 1, 1)
-        relax(4)
-        relax(5)
-        quantize_x(4)
-        quantize_x(5)
+        pair = relax_pair(4)
+        quantize_pair(4, pair)
         quantize_fresh(0, 1)
         quantize_fresh(1, 1)
         for i in (4, 5):
@@ -344,11 +351,9 @@ def tile_two_jacobi_sweeps_s10_kernel(
         for a in range(6, TILES, 2):
             turn(a)
             turn(a + 1)
-            relax(a)
-            relax(a + 1)
+            pair = relax_pair(a)
             finish(waiting[0], waiting[1])
-            quantize_x(a)
-            quantize_x(a + 1)
+            quantize_pair(a, pair)
             for i, h in order:
                 for part in range(3):
                     mm(i, h, part)
@@ -357,13 +362,16 @@ def tile_two_jacobi_sweeps_s10_kernel(
             waiting = order[-1]
             order = [(a, 0), (a + 1, 0), (a, 1), (a + 1, 1)]
         finish(waiting[0], waiting[1])
-        e2()
         for i, h in order[:3]:
             for part in range(3):
                 mm(i, h, part)
-            e1(i, h, 0, HALF)
-            e2()
+            finish(i, h)
         i, h = order[3]
-        for c in range(4):
-            quarter(i, h, c)
-        e2()
+        t = work.tile([P, HALF], F32, name="diff", bufs=8)
+        for c in range(3):
+            quarter(i, h, c, t)
+        late.append((t, i, h, 0, 256))
+        e2(nc.vector)
+        quarter(i, h, 3, t)
+        late.append((t, i, h, 256, 512))
+        e2(nc.vector)

@@ -42,6 +42,8 @@ def tile_two_jacobi_sweeps_s10_kernel(
         nc.vector.memset(near_sc[:].bitcast(I32), 0)
 
         r1c = keep.tile([P, G, 2, 2], BF16, name="r1c", align_bytes=64)
+        r1pad = keep.tile([P, P], F32, name="r1pad", align_bytes=64)
+        r1row = keep.tile([P, P], F32, name="r1row", align_bytes=64)
         r2c = keep.tile([P, 4, 2], BF16, name="r2c", align_bytes=64)
         r2 = keep.tile([P, N], F32, name="r2", align_bytes=64)
 
@@ -83,6 +85,22 @@ def tile_two_jacobi_sweeps_s10_kernel(
                 in_=fresh[g * 512 : (g + 1) * 512, h * HALF : (h + 1) * HALF].rearrange("(p j) n -> p j n", j=4),
             )
 
+        blocks = {}
+
+        def load_blocks(first, count):
+            t = keep.tile([P, G, 4 * count, P], BF16, name="blocks%d" % first, align_bytes=64)
+            for q in range(4):
+                for g in range(G):
+                    nc.sync.dma_start(
+                        out=t[32 * q : 32 * q + 32, g, :, :],
+                        in_=b[
+                            first * P : (first + count) * P,
+                            512 * g + P * q : 512 * g + P * (q + 1),
+                        ].rearrange("(j r) k -> r j k", r=32),
+                    )
+            for c in range(count):
+                blocks[first + c] = t[:, :, 4 * c : 4 * (c + 1), :]
+
         load_b(0, 1)
         nc.scalar.dma_start(
             out=r1c[:], in_=relax1.rearrange("(g p u e) -> p g u e", g=G, u=2, e=2)
@@ -90,20 +108,23 @@ def tile_two_jacobi_sweeps_s10_kernel(
         load_scales(nc.sync, far_sc, far_scales)
         load_b(1, 1)
         nc.sync.dma_start(out=far_sb[:], in_=far_words.rearrange("g p c -> p g c"))
-        nc.gpsimd.dma_start(
+        load_scales(nc.scalar, near_sc, near_scales)
+        load_b(2, 2)
+        nc.scalar.dma_start(
             out=r2c[:], in_=relax2.rearrange("(c p e) -> p c e", p=P, e=2)
         )
-        load_scales(nc.scalar, near_sc, near_scales)
         load_near(0)
-        load_b(2, 2)
+        load_b(4, 2)
+        load_near(1)
         load_fresh(0, 0)
         load_fresh(1, 0)
-        load_near(1)
-        load_b(4, 2)
         load_fresh(0, 1)
         load_fresh(1, 1)
-        for i in range(6, TILES, 2):
-            load_b(i, 2)
+        load_blocks(6, 2)
+        load_b(6, 2)
+        load_blocks(8, 4)
+        load_b(8, 2)
+        load_b(10, 2)
 
         words_in = {}
 
@@ -115,10 +136,28 @@ def tile_two_jacobi_sweeps_s10_kernel(
             )
             words_in[i] = t
 
+        shuffled = {}
         tr = {}
 
+        def shuffle(i):
+            t = work.tile([P, 2 * P * G], F32, name="shuf", align_bytes=64)
+            nc.scalar.copy(
+                out=t[:].rearrange("p (u g j a) -> p u g j a", u=2, g=G, j=4),
+                in_=blocks[i].bitcast(F32).rearrange("p g j (a u) -> p u g j a", u=2),
+            )
+            shuffled[i] = t
+
+        def turn_on_vector(i):
+            t = work.tile([P, 2 * P * G], F32, name="vturn", align_bytes=64)
+            nc.vector.transpose(out=t[:], in_=shuffled[i][:])
+            tr[i] = t
+
+
         def turn(i):
-            bank = turned.tile([P, 512], F32, name="turn")
+            if i < 4:
+                bank = turned.tile([P, 512], F32, name="turn")
+            else:
+                bank = sums.tile([P, 512], F32, name="acc")
             tr[i] = bank
             for g in range(G):
                 for u in range(2):
@@ -130,6 +169,7 @@ def tile_two_jacobi_sweeps_s10_kernel(
                         bank[:, u * 256 + g * P : u * 256 + (g + 1) * P], src, ident[:]
                     )
 
+        factor = [r1c[:]]
         xg = {}
         xc = {}
         xs = {}
@@ -146,7 +186,7 @@ def tile_two_jacobi_sweeps_s10_kernel(
                 in0=tr[i][:]
                 .bitcast(BF16)
                 .rearrange("p (u g m e) -> p g m u e", g=G, u=2, e=2)[:, part],
-                in1=r1c[:, part].unsqueeze(2).to_broadcast([P, n, P, 2, 2]),
+                in1=factor[0][:, part].unsqueeze(2).to_broadcast([P, n, P, 2, 2]),
                 op=ALU.mult,
             )
 
@@ -235,143 +275,137 @@ def tile_two_jacobi_sweeps_s10_kernel(
             )
             late.append((t, i, h, c0, c1))
 
-        def e2(eng=nc.gpsimd):
+        def e2(on_vector):
             t, i, h, c0, c1 = late[0]
             late.remove(late[0])
-            o = work.tile([P, HALF], F32, name="res", bufs=6)
-            eng.tensor_tensor(
-                out=o[:, c0:c1], in0=t[:, c0:c1], in1=r2[:, h * HALF + c0 : h * HALF + c1], op=ALU.mult
-            )
+            o = work.tile([P, HALF], F32, name="res", bufs=10)
+            cols = slice(h * HALF + c0, h * HALF + c1)
+            if on_vector:
+                nc.vector.tensor_tensor(out=o[:, c0:c1], in0=t[:, c0:c1], in1=r2_psum[:, cols], op=ALU.mult)
+            else:
+                nc.gpsimd.tensor_tensor(out=o[:, c0:c1], in0=t[:, c0:c1], in1=r2[:, cols], op=ALU.mult)
             nc.sync.dma_start(
                 out=out[i * P : (i + 1) * P, h * HALF + c0 : h * HALF + c1], in_=o[:, c0:c1]
             )
 
         def finish(i, h):
             e1(i, h, 0, HALF)
-            e2()
+            e2(i >= 10 or (i, h) in ((5, 1), (7, 1), (9, 1)))
 
-        def quarter(i, h, c, t):
-            bank = sums.tile([P, HALF], F32, name="acc")
-            for part in range(3):
-                for g in range(G):
-                    c0 = h * HALF + c * P
-                    if part == 0:
-                        rhs = far_sb[:, g, 2 * c0 : 2 * (c0 + P)].bitcast(FP4X4)
-                        sc = far_sc[:, g * N + c0 : g * N + c0 + P]
-                    elif part == 1:
-                        rhs = near[h][:, g, 4 * c * P : 4 * (c + 1) * P].bitcast(FP8X4)
-                        sc = near_sc[:, g * N + c0 : g * N + c0 + P]
-                    else:
-                        rhs = fc[g, h][:, c * P : (c + 1) * P].bitcast(FP8X4)
-                        sc = fs[g, h][:, c * P : (c + 1) * P]
-                    nc.tensor.matmul_mx(
-                        out=bank[:, 0:P],
-                        lhsT=xc[i][:, g * P : (g + 1) * P].bitcast(FP8X4),
-                        lhsT_scale=xs[i][:, g * P : (g + 1) * P],
-                        rhs=rhs,
-                        rhs_scale=sc,
-                        start=(part == 0 and g == 0),
-                        stop=(part == 2 and g == 1),
-                    )
-            nc.vector.scalar_tensor_tensor(
-                out=t[:, c * P : (c + 1) * P],
-                in0=b_sb[i][:, h * HALF + c * P : h * HALF + (c + 1) * P],
-                scalar=CENTRE,
-                in1=bank[:, 0:P],
-                op0=ALU.mult,
-                op1=ALU.subtract,
-            )
-
+        nc.vector.memset(r1pad[:], 0.0)
+        nc.vector.tensor_copy(out=r1pad[:, 0:4], in_=r1c[:].rearrange("p g u e -> p (g u e)").bitcast(F32))
         turn(0)
         relax(0, (0, 1))
         relax(0, (1, 2))
         quantize_x(0, (0, 1))
         quantize_x(0, (1, 2))
         turn(1)
+        bank2 = sums.tile([P, 512], F32, name="acc")
+        nc.tensor.transpose(bank2[:, 0:P], r1pad[:], ident[:])
+        nc.scalar.copy(out=r1row[:], in_=bank2[:, 0:P])
         relax(1)
         quantize_x(1)
-        mm(0, 0, 0)
-        mm(1, 0, 0)
+        for i in range(2):
+            mm(i, 0, 0)
+            mm(i, 1, 0)
+        permute(2)
+        permute(3)
         turn(2)
         turn(3)
-        bank = sums.tile([P, 512], F32, name="acc")
-        for c in range(4):
-            nc.tensor.transpose(
-                bank[:, c * P : (c + 1) * P],
-                r2c[:].rearrange("p c e -> p (c e)").bitcast(F32)[:, c : c + 1].to_broadcast([P, P]),
-                ident[:],
-            )
+        turn(4)
+        turn(5)
         relax(2)
         relax(3)
+        pair4 = relax_pair(4)
         quantize_x(2)
         quantize_x(3)
         interleave(nc.scalar.copy, 0, 0)
-        nc.scalar.copy(out=r2[:], in_=bank[:].bitcast(BF16))
         interleave(nc.vector.tensor_copy, 1, 0)
         quantize_fresh(0, 0)
         quantize_fresh(1, 0)
-        mm(0, 0, 1)
-        mm(1, 0, 1)
+        for h in range(2):
+            for i in range(2):
+                mm(i, h, 1)
+        bank3 = turned.tile([P, 512], F32, name="turn")
+        nc.tensor.transpose(bank3[:, 0:P], r1row[:], ident[:])
+        factor[0] = bank3[:, 0:4].bitcast(BF16).rearrange("p (g u e) -> p g u e", g=G, u=2)
+        bank4 = turned.tile([P, 512], F32, name="turn")
+        for c in range(4):
+            nc.tensor.transpose(
+                bank4[:, c * P : (c + 1) * P],
+                r2c[:].rearrange("p c e -> p (c e)").bitcast(F32)[:, c : c + 1].to_broadcast([P, P]),
+                ident[:],
+            )
+        r2_psum = bank4[:].bitcast(BF16)
         for i in (2, 3):
             mm(i, 0, 0)
             mm(i, 0, 1)
-        permute(4)
-        permute(5)
+        nc.scalar.copy(out=r2[:], in_=r2_psum)
         interleave(nc.scalar.copy, 0, 1)
         interleave(nc.scalar.copy, 1, 1)
+        pieces = []
 
-        for i in range(2):
-            mm(i, 1, 0)
+        def plan(a):
+            def multiply(i):
+                if i == a:
+                    xg2[a] = work.tile([P, 2, G * P * 4], BF16, name="xg2", align_bytes=64, bufs=2)
+                    xg[a] = xg2[a][:, 0, :]
+                    xg[a + 1] = xg2[a][:, 1, :]
+                relax(i)
+
+            pieces.extend(
+                [
+                    lambda: turn_on_vector(a),
+                    lambda: turn_on_vector(a + 1),
+                    lambda: multiply(a),
+                    lambda: multiply(a + 1),
+                    lambda: quantize_pair(a, xg2[a]),
+                ]
+            )
+
+        def step():
+            if pieces:
+                piece = pieces[0]
+                pieces.remove(piece)
+                piece()
+
+        xg2 = {}
+        for a in range(6, TILES, 2):
+            plan(a)
+
+        quantize_pair(4, pair4)
         for i in range(4):
             mm(i, 0, 2)
             finish(i, 0)
-        turn(4)
-        turn(5)
-        for i in range(2):
-            mm(i, 1, 1)
+        for i in range(6, TILES):
+            shuffle(i)
         for i in (2, 3):
             mm(i, 1, 0)
             mm(i, 1, 1)
-        pair = relax_pair(4)
-        quantize_pair(4, pair)
         quantize_fresh(0, 1)
         quantize_fresh(1, 1)
+        step()
+        step()
         for i in (4, 5):
             for part in range(3):
                 mm(i, 0, part)
             finish(i, 0)
-        for i in range(6, TILES):
-            permute(i)
         for i in range(4):
             mm(i, 1, 2)
-            if i < 3:
-                finish(i, 1)
-        waiting = (3, 1)
-        order = [(4, 1), (5, 1)]
-        for a in range(6, TILES, 2):
-            turn(a)
-            turn(a + 1)
-            pair = relax_pair(a)
-            finish(waiting[0], waiting[1])
-            quantize_pair(a, pair)
-            for i, h in order:
-                for part in range(3):
-                    mm(i, h, part)
-                if (i, h) != order[-1]:
-                    finish(i, h)
-            waiting = order[-1]
-            order = [(a, 0), (a + 1, 0), (a, 1), (a + 1, 1)]
-        finish(waiting[0], waiting[1])
-        for i, h in order[:3]:
+            finish(i, 1)
+            step()
+        order = [(4, 1), (5, 1)] + [(a + c, h) for a in range(6, TILES, 2) for h in range(2) for c in range(2)]
+        for i, h in order[:-1]:
             for part in range(3):
                 mm(i, h, part)
             finish(i, h)
-        i, h = order[3]
-        t = work.tile([P, HALF], F32, name="diff", bufs=8)
-        for c in range(3):
-            quarter(i, h, c, t)
-        late.append((t, i, h, 0, 256))
-        e2(nc.vector)
-        quarter(i, h, 3, t)
-        late.append((t, i, h, 256, 512))
-        e2(nc.vector)
+            step()
+            if i < 6:
+                step()
+        i, h = order[-1]
+        for part in range(3):
+            mm(i, h, part)
+        e1(i, h, 0, 256)
+        e1(i, h, 256, 512)
+        e2(True)
+        e2(True)

from contextlib import ExitStack

import concourse.mybir as mybir
from concourse.masks import make_identity

M, N = 1536, 1024
CENTRE = 1.6
FLOPS = 3 * 2 * M * N * N

F32 = mybir.dt.float32
BF16 = mybir.dt.bfloat16
I32 = mybir.dt.int32
U32 = mybir.dt.uint32
U8 = mybir.dt.uint8
FP8X4 = mybir.dt.float8_e4m3fn_x4
FP4X4 = mybir.dt.float4_e2m1fn_x4
ALU = mybir.AluOpType

P = 128
G = 2
HALF = 512
TILES = M // P


def tile_two_jacobi_sweeps_s10_kernel(
    tc, b, relax1, relax2, far_words, far_scales, near_words, near_scales, fresh, out
):
    nc = tc.nc
    with ExitStack() as ctx:
        keep = ctx.enter_context(tc.tile_pool(name="keep", bufs=1))
        work = ctx.enter_context(tc.tile_pool(name="work", bufs=3))
        turned = ctx.enter_context(tc.psum_pool(name="turned", bufs=2))
        sums = ctx.enter_context(tc.psum_pool(name="sums", bufs=6))
        ctx.enter_context(tc.manual_schedule())

        ident = keep.tile([P, P], F32, name="ident")
        make_identity(nc, ident[:])

        far_sc = keep.tile([P, G * N], U8, name="far_sc", align_bytes=64)
        near_sc = keep.tile([P, G * N], U8, name="near_sc", align_bytes=64)
        nc.vector.memset(far_sc[:].bitcast(I32), 0)
        nc.vector.memset(near_sc[:].bitcast(I32), 0)

        r1c = keep.tile([P, G, 2, 2], BF16, name="r1c", align_bytes=64)
        r1pad = keep.tile([P, P], F32, name="r1pad", align_bytes=64)
        r1row = keep.tile([P, P], F32, name="r1row", align_bytes=64)
        r2c = keep.tile([P, 4, 2], BF16, name="r2c", align_bytes=64)
        r2 = keep.tile([P, N], F32, name="r2", align_bytes=64)

        b_sb = {}

        def load_b(i, count):
            t = keep.tile([P, count, N], BF16, name="b%d" % i, align_bytes=64)
            nc.sync.dma_start(
                out=t[:], in_=b[i * P : (i + count) * P, :].rearrange("(c p) k -> p c k", p=P)
            )
            for c in range(count):
                b_sb[i + c] = t[:, c, :]

        def load_scales(eng, plane, dram):
            words = plane[:].bitcast(I32)
            src = dram.bitcast(I32)
            for q in range(4):
                eng.dma_start(
                    out=words[32 * q : 32 * q + 4, :].rearrange("r (g n) -> r g n", g=G),
                    in_=src[:, 4 * q : 4 * q + 4, :].rearrange("g r n -> r g n"),
                )

        near = {}
        raw = {}

        far_sb = keep.tile([P, G, 2 * N], U8, name="far_sb", align_bytes=64)

        def load_near(h):
            near[h] = keep.tile([P, G, 4 * HALF], U8, name="near%d" % h, align_bytes=64)
            nc.sync.dma_start(
                out=near[h][:],
                in_=near_words[:, :, h * HALF : (h + 1) * HALF, :].rearrange("g p n t -> p g (n t)"),
            )

        def load_fresh(g, h):
            raw[g, h] = keep.tile([P, 4, HALF], BF16, name="raw%d%d" % (g, h), align_bytes=64)
            nc.sync.dma_start(
                out=raw[g, h][:],
                in_=fresh[g * 512 : (g + 1) * 512, h * HALF : (h + 1) * HALF].rearrange("(p j) n -> p j n", j=4),
            )

        blocks = {}

        def load_blocks(first, count):
            t = keep.tile([P, G, 4 * count, P], BF16, name="blocks%d" % first, align_bytes=64)
            for q in range(4):
                for g in range(G):
                    nc.sync.dma_start(
                        out=t[32 * q : 32 * q + 32, g, :, :],
                        in_=b[
                            first * P : (first + count) * P,
                            512 * g + P * q : 512 * g + P * (q + 1),
                        ].rearrange("(j r) k -> r j k", r=32),
                    )
            for c in range(count):
                blocks[first + c] = t[:, :, 4 * c : 4 * (c + 1), :]

        load_b(0, 1)
        nc.scalar.dma_start(
            out=r1c[:], in_=relax1.rearrange("(g p u e) -> p g u e", g=G, u=2, e=2)
        )
        load_scales(nc.sync, far_sc, far_scales)
        load_b(1, 1)
        nc.sync.dma_start(out=far_sb[:], in_=far_words.rearrange("g p c -> p g c"))
        load_scales(nc.scalar, near_sc, near_scales)
        load_b(2, 2)
        nc.scalar.dma_start(
            out=r2c[:], in_=relax2.rearrange("(c p e) -> p c e", p=P, e=2)
        )
        load_near(0)
        load_b(4, 2)
        load_near(1)
        load_fresh(0, 0)
        load_fresh(1, 0)
        load_fresh(0, 1)
        load_fresh(1, 1)
        load_blocks(6, 2)
        load_b(6, 2)
        load_blocks(8, 4)
        load_b(8, 2)
        load_b(10, 2)

        words_in = {}

        def permute(i):
            t = work.tile([P, 2 * P * G], F32, name="perm", align_bytes=64)
            nc.scalar.copy(
                out=t[:].rearrange("m (g u p) -> m g u p", g=G, u=2),
                in_=b_sb[i].bitcast(F32).rearrange("m (g p u) -> m g u p", g=G, u=2),
            )
            words_in[i] = t

        shuffled = {}
        tr = {}

        def shuffle(i):
            t = work.tile([P, 2 * P * G], F32, name="shuf", align_bytes=64)
            nc.scalar.copy(
                out=t[:].rearrange("p (u g j a) -> p u g j a", u=2, g=G, j=4),
                in_=blocks[i].bitcast(F32).rearrange("p g j (a u) -> p u g j a", u=2),
            )
            shuffled[i] = t

        def turn_on_vector(i):
            t = work.tile([P, 2 * P * G], F32, name="vturn", align_bytes=64)
            nc.vector.transpose(out=t[:], in_=shuffled[i][:])
            tr[i] = t


        def turn(i):
            if i < 4:
                bank = turned.tile([P, 512], F32, name="turn")
            else:
                bank = sums.tile([P, 512], F32, name="acc")
            tr[i] = bank
            for g in range(G):
                for u in range(2):
                    if i in words_in:
                        src = words_in[i][:, (2 * g + u) * P : (2 * g + u + 1) * P]
                    else:
                        src = b_sb[i].bitcast(F32)[:, 256 * g + u : 256 * (g + 1) : 2]
                    nc.tensor.transpose(
                        bank[:, u * 256 + g * P : u * 256 + (g + 1) * P], src, ident[:]
                    )

        factor = [r1c[:]]
        xg = {}
        xc = {}
        xs = {}

        def relax(i, gs=(0, G)):
            if i not in xg:
                xg[i] = work.tile([P, G * P * 4], BF16, name="xg", align_bytes=64)
            n = gs[1] - gs[0]
            part = slice(gs[0], gs[1])
            nc.vector.tensor_tensor(
                out=xg[i][:, gs[0] * 512 : gs[1] * 512].rearrange(
                    "p (g m u e) -> p g m u e", g=n, u=2, e=2
                ),
                in0=tr[i][:]
                .bitcast(BF16)
                .rearrange("p (u g m e) -> p g m u e", g=G, u=2, e=2)[:, part],
                in1=factor[0][:, part].unsqueeze(2).to_broadcast([P, n, P, 2, 2]),
                op=ALU.mult,
            )

        def quantize_x(i, gs=(0, G)):
            if gs[0] == 0:
                xc[i] = keep.tile([P, G * P], U32, name="xc%d" % i, align_bytes=64)
                xs[i] = keep.tile([P, G * P], U8, name="xs%d" % i, align_bytes=64)
            cols = slice(gs[0] * P, gs[1] * P)
            nc.vector.quantize_mx(
                out=xc[i][:, cols].bitcast(FP8X4),
                scales=xs[i][:, cols],
                in_=xg[i][:, gs[0] * 512 : gs[1] * 512],
            )

        def relax_pair(a):
            t = work.tile([P, 2, G * P * 4], BF16, name="xg2", align_bytes=64, bufs=2)
            xg[a] = t[:, 0, :]
            xg[a + 1] = t[:, 1, :]
            relax(a)
            relax(a + 1)
            return t

        def quantize_pair(a, t):
            c = keep.tile([P, 2 * G * P], U32, name="xc%d" % a, align_bytes=64)
            s = keep.tile([P, 2 * G * P], U8, name="xs%d" % a, align_bytes=64)
            nc.vector.quantize_mx(
                out=c[:].bitcast(FP8X4), scales=s[:], in_=t[:].rearrange("p c w -> p (c w)")
            )
            for k in range(2):
                xc[a + k] = c[:, k * G * P : (k + 1) * G * P]
                xs[a + k] = s[:, k * G * P : (k + 1) * G * P]

        fi = {}
        fc = {}
        fs = {}

        def interleave(eng_copy, g, h):
            t = work.tile([P, 4 * HALF], BF16, name="fi", align_bytes=64)
            eng_copy(
                out=t[:].rearrange("p (c i j) -> p c j i", i=4, j=4),
                in_=raw[g, h][:].rearrange("p j (c i) -> p c j i", i=4),
            )
            fi[g, h] = t

        def quantize_fresh(g, h):
            fc[g, h] = keep.tile([P, HALF], U32, name="fc%d%d" % (g, h), align_bytes=64)
            fs[g, h] = keep.tile([P, HALF], U8, name="fs%d%d" % (g, h), align_bytes=64)
            nc.vector.quantize_mx(out=fc[g, h][:].bitcast(FP8X4), scales=fs[g, h][:], in_=fi[g, h][:])

        acc = {}

        def mm(i, h, part):
            if part == 0:
                acc[i, h] = sums.tile([P, HALF], F32, name="acc")
            for g in range(G):
                if part == 0:
                    rhs = far_sb[:, g, h * N : (h + 1) * N].bitcast(FP4X4)
                    sc = far_sc[:, g * N + h * HALF : g * N + (h + 1) * HALF]
                elif part == 1:
                    rhs = near[h][:, g, :].bitcast(FP8X4)
                    sc = near_sc[:, g * N + h * HALF : g * N + (h + 1) * HALF]
                else:
                    rhs = fc[g, h][:].bitcast(FP8X4)
                    sc = fs[g, h][:]
                nc.tensor.matmul_mx(
                    out=acc[i, h][:],
                    lhsT=xc[i][:, g * P : (g + 1) * P].bitcast(FP8X4),
                    lhsT_scale=xs[i][:, g * P : (g + 1) * P],
                    rhs=rhs,
                    rhs_scale=sc,
                    start=(part == 0 and g == 0),
                    stop=(part == 2 and g == 1),
                )

        late = []

        def e1(i, h, c0, c1):
            t = work.tile([P, HALF], F32, name="diff", bufs=8)
            nc.vector.scalar_tensor_tensor(
                out=t[:, c0:c1],
                in0=b_sb[i][:, h * HALF + c0 : h * HALF + c1],
                scalar=CENTRE,
                in1=acc[i, h][:, c0:c1],
                op0=ALU.mult,
                op1=ALU.subtract,
            )
            late.append((t, i, h, c0, c1))

        def e2(on_vector):
            t, i, h, c0, c1 = late[0]
            late.remove(late[0])
            o = work.tile([P, HALF], F32, name="res", bufs=10)
            cols = slice(h * HALF + c0, h * HALF + c1)
            if on_vector:
                nc.vector.tensor_tensor(out=o[:, c0:c1], in0=t[:, c0:c1], in1=r2_psum[:, cols], op=ALU.mult)
            else:
                nc.gpsimd.tensor_tensor(out=o[:, c0:c1], in0=t[:, c0:c1], in1=r2[:, cols], op=ALU.mult)
            nc.sync.dma_start(
                out=out[i * P : (i + 1) * P, h * HALF + c0 : h * HALF + c1], in_=o[:, c0:c1]
            )

        def finish(i, h):
            e1(i, h, 0, HALF)
            e2(i >= 10 or (i, h) in ((5, 1), (7, 1), (9, 1)))

        nc.vector.memset(r1pad[:], 0.0)
        nc.vector.tensor_copy(out=r1pad[:, 0:4], in_=r1c[:].rearrange("p g u e -> p (g u e)").bitcast(F32))
        turn(0)
        relax(0, (0, 1))
        relax(0, (1, 2))
        quantize_x(0, (0, 1))
        quantize_x(0, (1, 2))
        turn(1)
        bank2 = sums.tile([P, 512], F32, name="acc")
        nc.tensor.transpose(bank2[:, 0:P], r1pad[:], ident[:])
        nc.scalar.copy(out=r1row[:], in_=bank2[:, 0:P])
        relax(1)
        quantize_x(1)
        for i in range(2):
            mm(i, 0, 0)
            mm(i, 1, 0)
        permute(2)
        permute(3)
        turn(2)
        turn(3)
        turn(4)
        turn(5)
        relax(2)
        relax(3)
        pair4 = relax_pair(4)
        quantize_x(2)
        quantize_x(3)
        interleave(nc.scalar.copy, 0, 0)
        interleave(nc.vector.tensor_copy, 1, 0)
        quantize_fresh(0, 0)
        quantize_fresh(1, 0)
        for h in range(2):
            for i in range(2):
                mm(i, h, 1)
        bank3 = turned.tile([P, 512], F32, name="turn")
        nc.tensor.transpose(bank3[:, 0:P], r1row[:], ident[:])
        factor[0] = bank3[:, 0:4].bitcast(BF16).rearrange("p (g u e) -> p g u e", g=G, u=2)
        bank4 = turned.tile([P, 512], F32, name="turn")
        for c in range(4):
            nc.tensor.transpose(
                bank4[:, c * P : (c + 1) * P],
                r2c[:].rearrange("p c e -> p (c e)").bitcast(F32)[:, c : c + 1].to_broadcast([P, P]),
                ident[:],
            )
        r2_psum = bank4[:].bitcast(BF16)
        for i in (2, 3):
            mm(i, 0, 0)
            mm(i, 0, 1)
        nc.scalar.copy(out=r2[:], in_=r2_psum)
        interleave(nc.scalar.copy, 0, 1)
        interleave(nc.scalar.copy, 1, 1)
        pieces = []

        def plan(a):
            def multiply(i):
                if i == a:
                    xg2[a] = work.tile([P, 2, G * P * 4], BF16, name="xg2", align_bytes=64, bufs=2)
                    xg[a] = xg2[a][:, 0, :]
                    xg[a + 1] = xg2[a][:, 1, :]
                relax(i)

            pieces.extend(
                [
                    lambda: turn_on_vector(a),
                    lambda: turn_on_vector(a + 1),
                    lambda: multiply(a),
                    lambda: multiply(a + 1),
                    lambda: quantize_pair(a, xg2[a]),
                ]
            )

        def step():
            if pieces:
                piece = pieces[0]
                pieces.remove(piece)
                piece()

        xg2 = {}
        for a in range(6, TILES, 2):
            plan(a)

        quantize_pair(4, pair4)
        for i in range(4):
            mm(i, 0, 2)
            finish(i, 0)
        for i in range(6, TILES):
            shuffle(i)
        for i in (2, 3):
            mm(i, 1, 0)
            mm(i, 1, 1)
        quantize_fresh(0, 1)
        quantize_fresh(1, 1)
        step()
        step()
        for i in (4, 5):
            for part in range(3):
                mm(i, 0, part)
            finish(i, 0)
        for i in range(4):
            mm(i, 1, 2)
            finish(i, 1)
            step()
        order = [(4, 1), (5, 1)] + [(a + c, h) for a in range(6, TILES, 2) for h in range(2) for c in range(2)]
        for i, h in order[:-1]:
            for part in range(3):
                mm(i, h, part)
            finish(i, h)
            step()
            if i < 6:
                step()
        i, h = order[-1]
        for part in range(3):
            mm(i, h, part)
        e1(i, h, 0, 256)
        e1(i, h, 256, 512)
        e2(True)
        e2(True)
